import numpy as np
import ml_dtypes


def mxq(x, axis, fmt="e4m3"):
    dtype, down = {"e4m3": (ml_dtypes.float8_e4m3fn, 7), "e5m2": (ml_dtypes.float8_e5m2, 14)}[fmt]
    v = np.moveaxis(np.asarray(x, np.float32).astype(ml_dtypes.bfloat16).astype(np.float64), axis, -1)
    blocks = v.reshape(v.shape[:-1] + (-1, 32))
    amax = np.abs(blocks).max(-1, keepdims=True)
    byte = np.maximum(np.where(amax > 0, np.frexp(amax)[1] - 1 + 127, 0) - down, 1)
    scale = np.exp2(byte - 127.0)
    codes = (blocks / scale).astype(np.float32).astype(dtype).astype(np.float64)
    return np.moveaxis((codes * scale).reshape(v.shape), -1, axis)


WIDE = False


def mx_kscale(k):
    if not WIDE:
        return np.ones(k)
    levels = np.array([30, -30])
    if k % 512:
        return np.exp2(np.random.permutation(np.resize(levels, k // 32))).repeat(32)
    a = np.empty((k // 512, 16))
    for p in range(k // 512):
        a[p, :8] = np.random.permutation(np.resize(levels, 8))
        for g in range(8):
            far = levels[np.abs(levels - a[p, g]) >= 10]
            a[p, g + 8] = far[np.random.randint(len(far))]
    return np.exp2(a.ravel()).repeat(32)


def f64(x):
    return np.asarray(x).astype(np.float64)


T, D, H = 2048, 1280, 512


def setup_inputs():
    n = np.random.standard_normal
    s1 = mx_kscale(T)[:, None]
    s2 = mx_kscale(T)[:, None]
    m = np.exp(0.5 * n((T, 1)))
    return {
        "x": (n((T, D)) * s1).astype(np.float32),
        "de": (m * n((T, H)) / np.sqrt(T) / s1).astype(np.float32),
        "dr": (m * n((T, D)) / np.sqrt(T) * s2).astype(np.float32),
        "e": (n((T, H)) / s2).astype(np.float32),
        "mom": (n((1280, 512))).astype(np.float32),
    }


def reference(x, de, dr, e, mom):
    x_ = mxq(f64(x), 0, "e4m3")
    de_ = mxq(f64(de), 0, "e5m2")
    dr_ = mxq(f64(dr), 0, "e5m2")
    e_ = mxq(f64(e), 0, "e4m3")
    y = x_.T @ de_ + dr_.T @ e_
    return 0.9 * f64(mom) + y

@@ -1,0 +1,158 @@
+from contextlib import ExitStack
+
+import concourse.mybir as mybir
+
+T, D, H = 2048, 1280, 512
+FLOPS = 2 * 2 * T * D * H
+
+F32 = mybir.dt.float32
+BF16 = mybir.dt.bfloat16
+U32 = mybir.dt.uint32
+U8 = mybir.dt.uint8
+E4M3 = mybir.dt.float8_e4m3fn_x4
+E5M2 = mybir.dt.float8_e5m2_x4
+
+P = 128
+PACK = 4
+T_CHUNK = P * PACK
+MAIN_TILES = 8
+D_TILES = D // P
+MAIN = MAIN_TILES * P
+SIDE = D - MAIN
+RAW_BUFS = 4
+DECAY = 0.9
+
+CHUNKS = [(0, 0), (0, 1), (0, 2), (0, 3), (1, 0), (1, 1), (1, 3), (1, 2)]
+SPLIT = CHUNKS.index((1, 3))
+LAST = len(CHUNKS) - 1
+LAST_SCALAR_COLUMNS = 256
+
+
+def tile_mix_tied_ema_kernel(tc, x, de, dr, e, mom, out):
+    nc = tc.nc
+    products = [(x, E4M3, de, E5M2), (dr, E5M2, e, E4M3)]
+
+    with ExitStack() as ctx:
+        raw = ctx.enter_context(tc.tile_pool(name="raw", bufs=RAW_BUFS))
+        stage = ctx.enter_context(tc.tile_pool(name="stage", bufs=2))
+        codes = ctx.enter_context(tc.tile_pool(name="codes", bufs=3))
+        keep = ctx.enter_context(tc.tile_pool(name="keep", bufs=1))
+        psum = ctx.enter_context(tc.psum_pool(name="psum", bufs=1))
+        ctx.enter_context(tc.manual_schedule())
+
+        narrow_codes = keep.tile([P, len(CHUNKS), H], U32, align_bytes=64)
+        narrow_scales = keep.tile([P, len(CHUNKS), H], U8, align_bytes=64)
+        side_codes = keep.tile([P, len(CHUNKS), SIDE], U32, align_bytes=64)
+        side_scales = keep.tile([P, len(CHUNKS), SIDE], U8, align_bytes=64)
+        result = keep.tile([P, D_TILES, H], F32)
+        mom_tiles = mom.rearrange("(c p) h -> p c h", p=P)
+        out_tiles = out.rearrange("(c p) h -> p c h", p=P)
+
+        def rows_of(i, operand):
+            block = CHUNKS[i][1]
+            return operand[block * T_CHUNK : (block + 1) * T_CHUNK, :].rearrange("(p j) w -> p j w", j=PACK)
+
+        def load_chunk(i):
+            wide, wide_format, narrow, narrow_format = products[CHUNKS[i][0]]
+            raw_narrow = raw.tile([P, PACK, H], F32, name="raw_narrow")
+            nc.sync.dma_start(out=raw_narrow[:], in_=rows_of(i, narrow))
+            raw_wide = raw.tile([P, PACK, D], F32, name="raw_wide")
+            width = MAIN if i == SPLIT else D
+            nc.sync.dma_start(out=raw_wide[:, :, 0:width], in_=rows_of(i, wide)[:, :, 0:width])
+            return raw_narrow, raw_wide
+
+        def interleave(copy, grouped, source):
+            copy(out=grouped, in_=source.rearrange("p j w -> p w j"))
+
+        def quantize(format_x4, codes_view, scales_view, grouped):
+            nc.vector.quantize_mx(
+                out=codes_view.bitcast(format_x4),
+                scales=scales_view,
+                in_=grouped.rearrange("p w j -> p (w j)"),
+            )
+
+        def multiply(acc, i, wide_codes, wide_scales, start, stop):
+            wide, wide_format, narrow, narrow_format = products[CHUNKS[i][0]]
+            nc.tensor.matmul_mx(
+                out=acc[:],
+                lhsT=wide_codes.bitcast(wide_format),
+                lhsT_scale=wide_scales,
+                rhs=narrow_codes[:, i, :].bitcast(narrow_format),
+                rhs_scale=narrow_scales[:, i, :],
+                start=start,
+                stop=stop,
+            )
+
+        def finish(acc, c):
+            nc.vector.scalar_tensor_tensor(
+                out=result[:, c, :],
+                in0=result[:, c, :],
+                scalar=DECAY,
+                in1=acc[:],
+                op0=mybir.AluOpType.mult,
+                op1=mybir.AluOpType.add,
+            )
+
+        def load_mom(c0, c1):
+            nc.sync.dma_start(out=result[:, c0:c1, :], in_=mom_tiles[:, c0:c1, :])
+
+        def store(c0, c1):
+            nc.sync.dma_start(out=out_tiles[:, c0:c1, :], in_=result[:, c0:c1, :])
+
+        main_acc = [psum.tile([P, H], F32, name="bank%d" % c) for c in range(MAIN_TILES)]
+        loaded = {i: load_chunk(i) for i in range(RAW_BUFS)}
+
+        for i in range(len(CHUNKS)):
+            wide, wide_format, narrow, narrow_format = products[CHUNKS[i][0]]
+            raw_narrow, raw_wide = loaded[i]
+
+            narrow_grouped = stage.tile([P, H, PACK], BF16, name="narrow_grouped", align_bytes=64)
+            interleave(nc.scalar.copy, narrow_grouped[:], raw_narrow[:])
+            if i != SPLIT:
+                side_grouped = stage.tile([P, SIDE, PACK], BF16, name="side_grouped", align_bytes=64)
+                interleave(nc.scalar.copy, side_grouped[:], raw_wide[:, :, MAIN:D])
+            main_grouped = stage.tile([P, MAIN, PACK], BF16, name="main_grouped", align_bytes=64)
+            vector_from = LAST_SCALAR_COLUMNS if i == LAST else 0
+            if vector_from:
+                interleave(nc.scalar.copy, main_grouped[:, 0:vector_from, :], raw_wide[:, :, 0:vector_from])
+            interleave(nc.vector.tensor_copy, main_grouped[:, vector_from:MAIN, :], raw_wide[:, :, vector_from:MAIN])
+
+            if i + RAW_BUFS <= LAST:
+                loaded[i + RAW_BUFS] = load_chunk(i + RAW_BUFS)
+
+            main_codes = codes.tile([P, MAIN], U32, name="main_codes", align_bytes=64)
+            main_scales = codes.tile([P, MAIN], U8, name="main_scales", align_bytes=64)
+            quantize(narrow_format, narrow_codes[:, i, :], narrow_scales[:, i, :], narrow_grouped[:])
+            if i != SPLIT:
+                quantize(wide_format, side_codes[:, i, :], side_scales[:, i, :], side_grouped[:])
+            quantize(wide_format, main_codes[:], main_scales[:], main_grouped[:])
+
+            for c in range(MAIN_TILES):
+                d = slice(c * P, (c + 1) * P)
+                multiply(main_acc[c], i, main_codes[:, d], main_scales[:, d], start=(i == 0), stop=(i == LAST))
+
+        load_mom(0, 4)
+        wide, wide_format, narrow, narrow_format = products[CHUNKS[SPLIT][0]]
+        raw_side = keep.tile([P, PACK, SIDE], F32)
+        nc.sync.dma_start(out=raw_side[:], in_=rows_of(SPLIT, wide)[:, :, MAIN:D])
+        load_mom(4, MAIN_TILES)
+        load_mom(MAIN_TILES, D_TILES)
+
+        side_grouped = stage.tile([P, SIDE, PACK], BF16, name="side_grouped", align_bytes=64)
+        interleave(nc.scalar.copy, side_grouped[:], raw_side[:])
+        for c in range(D_TILES - MAIN_TILES):
+            finish(main_acc[c], c)
+        quantize(wide_format, side_codes[:, SPLIT, :], side_scales[:, SPLIT, :], side_grouped[:])
+        for c in range(D_TILES - MAIN_TILES, MAIN_TILES):
+            finish(main_acc[c], c)
+
+        for c in range(MAIN_TILES, D_TILES):
+            d = slice(c * P - MAIN, (c + 1) * P - MAIN)
+            acc = psum.tile([P, H], F32, name="bank%d" % (c - MAIN_TILES))
+            for i in range(len(CHUNKS)):
+                multiply(acc, i, side_codes[:, i, d], side_scales[:, i, d], start=(i == 0), stop=(i == LAST))
+            finish(acc, c)
+
+        store(0, 4)
+        store(4, MAIN_TILES)
+        store(MAIN_TILES, D_TILES)

@@ -15,17 +15,20 @@ E5M2 = mybir.dt.float8_e5m2_x4
 P = 128
 PACK = 4
 T_CHUNK = P * PACK
-MAIN_TILES = 8
+BLOCKS = T // T_CHUNK
 D_TILES = D // P
-MAIN = MAIN_TILES * P
-SIDE = D - MAIN
-RAW_BUFS = 4
 DECAY = 0.9
+RAW_BUFS = 4
 
-CHUNKS = [(0, 0), (0, 1), (0, 2), (0, 3), (1, 0), (1, 1), (1, 3), (1, 2)]
-SPLIT = CHUNKS.index((1, 3))
+GROUPS = [(0, 2), (2, 2), (4, 4), (8, 2)]
+FIRST_PAIR = [0, 1]
+LAST_PAIR = [8, 9]
+MIDDLE = list(range(2, 8))
+MAIN = 8 * P
+
+CHUNKS = [(product, block) for product in range(2) for block in range(BLOCKS)]
 LAST = len(CHUNKS) - 1
-LAST_SCALAR_COLUMNS = 256
+SWAP = LAST - 2
 
 
 def tile_mix_tied_ema_kernel(tc, x, de, dr, e, mom, out):
@@ -35,124 +38,180 @@ def tile_mix_tied_ema_kernel(tc, x, de, dr, e, mom, out):
     with ExitStack() as ctx:
         raw = ctx.enter_context(tc.tile_pool(name="raw", bufs=RAW_BUFS))
         stage = ctx.enter_context(tc.tile_pool(name="stage", bufs=2))
-        codes = ctx.enter_context(tc.tile_pool(name="codes", bufs=3))
         keep = ctx.enter_context(tc.tile_pool(name="keep", bufs=1))
         psum = ctx.enter_context(tc.psum_pool(name="psum", bufs=1))
         ctx.enter_context(tc.manual_schedule())
 
         narrow_codes = keep.tile([P, len(CHUNKS), H], U32, align_bytes=64)
         narrow_scales = keep.tile([P, len(CHUNKS), H], U8, align_bytes=64)
-        side_codes = keep.tile([P, len(CHUNKS), SIDE], U32, align_bytes=64)
-        side_scales = keep.tile([P, len(CHUNKS), SIDE], U8, align_bytes=64)
+        wide_codes = keep.tile([P, len(CHUNKS), D], U32, align_bytes=64)
+        wide_scales = keep.tile([P, len(CHUNKS), D], U8, align_bytes=64)
         result = keep.tile([P, D_TILES, H], F32)
-        mom_tiles = mom.rearrange("(c p) h -> p c h", p=P)
-        out_tiles = out.rearrange("(c p) h -> p c h", p=P)
+        raw_narrow = {}
+        raw_wide = {}
+        grouped_narrow = {}
+        grouped_wide = {}
 
         def rows_of(i, operand):
             block = CHUNKS[i][1]
             return operand[block * T_CHUNK : (block + 1) * T_CHUNK, :].rearrange("(p j) w -> p j w", j=PACK)
 
-        def load_chunk(i):
-            wide, wide_format, narrow, narrow_format = products[CHUNKS[i][0]]
-            raw_narrow = raw.tile([P, PACK, H], F32, name="raw_narrow")
-            nc.sync.dma_start(out=raw_narrow[:], in_=rows_of(i, narrow))
-            raw_wide = raw.tile([P, PACK, D], F32, name="raw_wide")
-            width = MAIN if i == SPLIT else D
-            nc.sync.dma_start(out=raw_wide[:, :, 0:width], in_=rows_of(i, wide)[:, :, 0:width])
-            return raw_narrow, raw_wide
+        def load_narrow(i):
+            narrow_raw = raw.tile([P, PACK, H], F32, name="narrow_raw")
+            nc.sync.dma_start(out=narrow_raw[:], in_=rows_of(i, products[CHUNKS[i][0]][2]))
+            raw_narrow[i] = narrow_raw
 
-        def interleave(copy, grouped, source):
-            copy(out=grouped, in_=source.rearrange("p j w -> p w j"))
+        def load_wide(i):
+            wide_raw = raw.tile([P, PACK, D], F32, name="wide_raw")
+            nc.sync.dma_start(out=wide_raw[:], in_=rows_of(i, products[CHUNKS[i][0]][0]))
+            raw_wide[i] = wide_raw
 
-        def quantize(format_x4, codes_view, scales_view, grouped):
-            nc.vector.quantize_mx(
-                out=codes_view.bitcast(format_x4),
-                scales=scales_view,
-                in_=grouped.rearrange("p w j -> p (w j)"),
+        def group_rows(hbm, g):
+            c, n = GROUPS[g]
+            return hbm[c * P : (c + n) * P, :].rearrange("(m c) h -> m c h", c=n)
+
+        def load_mom(g):
+            c, n = GROUPS[g]
+            nc.sync.dma_start(out=result[:, c : c + n, :], in_=group_rows(mom, g))
+
+        def store(g, c0, c1):
+            first = GROUPS[g][0]
+            nc.sync.dma_start(out=group_rows(out, g)[:, c0 - first : c1 - first, :], in_=result[:, c0:c1, :])
+
+        def cast_narrow(i):
+            narrow_grouped = stage.tile([P, H, PACK], BF16, name="narrow_grouped", align_bytes=64)
+            nc.scalar.copy(out=narrow_grouped[:], in_=raw_narrow[i][:].rearrange("p j w -> p w j"))
+            grouped_narrow[i] = narrow_grouped
+
+        def open_wide(i):
+            wide_grouped = stage.tile([P, D, PACK], BF16, name="wide_grouped", align_bytes=64)
+            grouped_wide[i] = wide_grouped
+
+        def cast_group(copy, i, g):
+            c, n = GROUPS[g]
+            w = slice(c * P, (c + n) * P)
+            copy(
+                out=grouped_wide[i][:, w, :].rearrange("p (c m) j -> p m c j", c=n),
+                in_=raw_wide[i][:, :, w].rearrange("p j (m c) -> p m c j", c=n),
             )
 
-        def multiply(acc, i, wide_codes, wide_scales, start, stop):
+        def quantize(format_x4, codes, scales, grouped):
+            nc.vector.quantize_mx(
+                out=codes.bitcast(format_x4), scales=scales, in_=grouped.rearrange("p w j -> p (w j)")
+            )
+
+        def quantize_narrow(i):
+            quantize(products[CHUNKS[i][0]][3], narrow_codes[:, i, :], narrow_scales[:, i, :], grouped_narrow[i][:])
+
+        def quantize_wide(i, w0, w1):
+            wide_format = products[CHUNKS[i][0]][1]
+            quantize(wide_format, wide_codes[:, i, w0:w1], wide_scales[:, i, w0:w1], grouped_wide[i][:, w0:w1, :])
+
+        def quantize_group(i, g):
+            c, n = GROUPS[g]
+            quantize_wide(i, c * P, (c + n) * P)
+
+        def multiply(c, i, start=False, stop=False):
             wide, wide_format, narrow, narrow_format = products[CHUNKS[i][0]]
+            d = slice(c * P, (c + 1) * P)
             nc.tensor.matmul_mx(
-                out=acc[:],
-                lhsT=wide_codes.bitcast(wide_format),
-                lhsT_scale=wide_scales,
+                out=acc[c][:],
+                lhsT=wide_codes[:, i, d].bitcast(wide_format),
+                lhsT_scale=wide_scales[:, i, d],
                 rhs=narrow_codes[:, i, :].bitcast(narrow_format),
                 rhs_scale=narrow_scales[:, i, :],
                 start=start,
                 stop=stop,
             )
 
-        def finish(acc, c):
+        def bank(b):
+            return psum.tile([P, H], F32, name="bank%d" % b)
+
+        def add_decayed(c):
             nc.vector.scalar_tensor_tensor(
                 out=result[:, c, :],
                 in0=result[:, c, :],
                 scalar=DECAY,
-                in1=acc[:],
+                in1=acc[c][:],
                 op0=mybir.AluOpType.mult,
                 op1=mybir.AluOpType.add,
             )
 
-        def load_mom(c0, c1):
-            nc.sync.dma_start(out=result[:, c0:c1, :], in_=mom_tiles[:, c0:c1, :])
+        def add_rest(c):
+            nc.vector.tensor_add(out=result[:, c, :], in0=result[:, c, :], in1=acc[c][:])
 
-        def store(c0, c1):
-            nc.sync.dma_start(out=out_tiles[:, c0:c1, :], in_=result[:, c0:c1, :])
+        acc = {c: bank(c) for c in MIDDLE}
+        for c in LAST_PAIR:
+            acc[c] = bank(c - 8)
+        for i in range(RAW_BUFS):
+            load_narrow(i)
+            load_wide(i)
 
-        main_acc = [psum.tile([P, H], F32, name="bank%d" % c) for c in range(MAIN_TILES)]
-        loaded = {i: load_chunk(i) for i in range(RAW_BUFS)}
-
-        for i in range(len(CHUNKS)):
-            wide, wide_format, narrow, narrow_format = products[CHUNKS[i][0]]
-            raw_narrow, raw_wide = loaded[i]
-
-            narrow_grouped = stage.tile([P, H, PACK], BF16, name="narrow_grouped", align_bytes=64)
-            interleave(nc.scalar.copy, narrow_grouped[:], raw_narrow[:])
-            if i != SPLIT:
-                side_grouped = stage.tile([P, SIDE, PACK], BF16, name="side_grouped", align_bytes=64)
-                interleave(nc.scalar.copy, side_grouped[:], raw_wide[:, :, MAIN:D])
-            main_grouped = stage.tile([P, MAIN, PACK], BF16, name="main_grouped", align_bytes=64)
-            vector_from = LAST_SCALAR_COLUMNS if i == LAST else 0
-            if vector_from:
-                interleave(nc.scalar.copy, main_grouped[:, 0:vector_from, :], raw_wide[:, :, 0:vector_from])
-            interleave(nc.vector.tensor_copy, main_grouped[:, vector_from:MAIN, :], raw_wide[:, :, vector_from:MAIN])
-
+        for i in range(LAST):
+            cast_narrow(i)
+            open_wide(i)
+            cast_group(nc.scalar.copy, i, 3)
+            for g in range(3):
+                cast_group(nc.vector.tensor_copy, i, g)
+            if i == 0:
+                load_mom(3)
             if i + RAW_BUFS <= LAST:
-                loaded[i + RAW_BUFS] = load_chunk(i + RAW_BUFS)
+                load_narrow(i + RAW_BUFS)
+                load_wide(i + RAW_BUFS)
 
-            main_codes = codes.tile([P, MAIN], U32, name="main_codes", align_bytes=64)
-            main_scales = codes.tile([P, MAIN], U8, name="main_scales", align_bytes=64)
-            quantize(narrow_format, narrow_codes[:, i, :], narrow_scales[:, i, :], narrow_grouped[:])
-            if i != SPLIT:
-                quantize(wide_format, side_codes[:, i, :], side_scales[:, i, :], side_grouped[:])
-            quantize(wide_format, main_codes[:], main_scales[:], main_grouped[:])
+            quantize_narrow(i)
+            quantize_wide(i, MAIN, D)
+            quantize_wide(i, 0, MAIN)
+            if i <= SWAP:
+                for c in LAST_PAIR:
+                    multiply(c, i, start=(i == 0), stop=(i == SWAP))
+            for c in MIDDLE:
+                multiply(c, i, start=(i == 0))
+            if i == SWAP:
+                for c in LAST_PAIR:
+                    add_decayed(c)
+                for c in FIRST_PAIR:
+                    acc[c] = bank(c)
+                    for k in range(SWAP + 1):
+                        multiply(c, k, start=(k == 0))
+            if i > SWAP:
+                for c in FIRST_PAIR:
+                    multiply(c, i)
 
-            for c in range(MAIN_TILES):
-                d = slice(c * P, (c + 1) * P)
-                multiply(main_acc[c], i, main_codes[:, d], main_scales[:, d], start=(i == 0), stop=(i == LAST))
+        for g in range(3):
+            load_mom(g)
 
-        load_mom(0, 4)
-        wide, wide_format, narrow, narrow_format = products[CHUNKS[SPLIT][0]]
-        raw_side = keep.tile([P, PACK, SIDE], F32)
-        nc.sync.dma_start(out=raw_side[:], in_=rows_of(SPLIT, wide)[:, :, MAIN:D])
-        load_mom(4, MAIN_TILES)
-        load_mom(MAIN_TILES, D_TILES)
-
-        side_grouped = stage.tile([P, SIDE, PACK], BF16, name="side_grouped", align_bytes=64)
-        interleave(nc.scalar.copy, side_grouped[:], raw_side[:])
-        for c in range(D_TILES - MAIN_TILES):
-            finish(main_acc[c], c)
-        quantize(wide_format, side_codes[:, SPLIT, :], side_scales[:, SPLIT, :], side_grouped[:])
-        for c in range(D_TILES - MAIN_TILES, MAIN_TILES):
-            finish(main_acc[c], c)
-
-        for c in range(MAIN_TILES, D_TILES):
-            d = slice(c * P - MAIN, (c + 1) * P - MAIN)
-            acc = psum.tile([P, H], F32, name="bank%d" % (c - MAIN_TILES))
-            for i in range(len(CHUNKS)):
-                multiply(acc, i, side_codes[:, i, d], side_scales[:, i, d], start=(i == 0), stop=(i == LAST))
-            finish(acc, c)
-
-        store(0, 4)
-        store(4, MAIN_TILES)
-        store(MAIN_TILES, D_TILES)
+        cast_narrow(LAST)
+        open_wide(LAST)
+        quantize_narrow(LAST)
+        cast_group(nc.vector.tensor_copy, LAST, 0)
+        cast_group(nc.scalar.copy, LAST, 1)
+        cast_group(nc.scalar.copy, LAST, 3)
+        quantize_group(LAST, 0)
+        cast_group(nc.vector.tensor_copy, LAST, 2)
+        for c in range(0, 2):
+            multiply(c, LAST, stop=True)
+        add_decayed(0)
+        quantize_group(LAST, 1)
+        for c in range(2, 4):
+            multiply(c, LAST, stop=True)
+        add_decayed(1)
+        store(0, 0, 2)
+        quantize_group(LAST, 2)
+        for c in range(4, 8):
+            multiply(c, LAST, stop=True)
+        add_decayed(2)
+        add_decayed(3)
+        store(1, 2, 4)
+        quantize_group(LAST, 3)
+        for c in LAST_PAIR:
+            acc[c] = bank(c - 8)
+            for i in range(SWAP + 1, LAST + 1):
+                multiply(c, i, start=(i == SWAP + 1), stop=(i == LAST))
+        for c in range(4, 8, 2):
+            add_decayed(c)
+            add_decayed(c + 1)
+            store(2, c, c + 2)
+        for c in LAST_PAIR:
+            add_rest(c)
+        store(3, 8, 10)

@@ -68,7 +68,7 @@ def tile_mix_tied_ema_kernel(tc, x, de, dr, e, mom, out):
 
         def group_rows(hbm, g):
             c, n = GROUPS[g]
-            return hbm[c * P : (c + n) * P, :].rearrange("(m c) h -> m c h", c=n)
+            return hbm[c * P : (c + n) * P, :].rearrange("(c p) h -> p c h", c=n)
 
         def load_mom(g):
             c, n = GROUPS[g]
@@ -78,22 +78,27 @@ def tile_mix_tied_ema_kernel(tc, x, de, dr, e, mom, out):
             first = GROUPS[g][0]
             nc.sync.dma_start(out=group_rows(out, g)[:, c0 - first : c1 - first, :], in_=result[:, c0:c1, :])
 
+        def interleave(copy, grouped, source):
+            copy(
+                out=grouped.rearrange("p (q i) j -> p q j i", i=4),
+                in_=source.rearrange("p j (q i) -> p q j i", i=4),
+            )
+
         def cast_narrow(i):
             narrow_grouped = stage.tile([P, H, PACK], BF16, name="narrow_grouped", align_bytes=64)
-            nc.scalar.copy(out=narrow_grouped[:], in_=raw_narrow[i][:].rearrange("p j w -> p w j"))
+            interleave(nc.scalar.copy, narrow_grouped[:], raw_narrow[i][:])
             grouped_narrow[i] = narrow_grouped
 
         def open_wide(i):
             wide_grouped = stage.tile([P, D, PACK], BF16, name="wide_grouped", align_bytes=64)
             grouped_wide[i] = wide_grouped
 
+        def cast_wide(copy, i, w0, w1):
+            interleave(copy, grouped_wide[i][:, w0:w1, :], raw_wide[i][:, :, w0:w1])
+
         def cast_group(copy, i, g):
             c, n = GROUPS[g]
-            w = slice(c * P, (c + n) * P)
-            copy(
-                out=grouped_wide[i][:, w, :].rearrange("p (c m) j -> p m c j", c=n),
-                in_=raw_wide[i][:, :, w].rearrange("p j (m c) -> p m c j", c=n),
-            )
+            cast_wide(copy, i, c * P, (c + n) * P)
 
         def quantize(format_x4, codes, scales, grouped):
             nc.vector.quantize_mx(
@@ -150,9 +155,8 @@ def tile_mix_tied_ema_kernel(tc, x, de, dr, e, mom, out):
         for i in range(LAST):
             cast_narrow(i)
             open_wide(i)
-            cast_group(nc.scalar.copy, i, 3)
-            for g in range(3):
-                cast_group(nc.vector.tensor_copy, i, g)
+            cast_wide(nc.scalar.copy, i, MAIN, D)
+            cast_wide(nc.vector.tensor_copy, i, 0, MAIN)
             if i == 0:
                 load_mom(3)
             if i + RAW_BUFS <= LAST:
@@ -186,21 +190,21 @@ def tile_mix_tied_ema_kernel(tc, x, de, dr, e, mom, out):
         quantize_narrow(LAST)
         cast_group(nc.vector.tensor_copy, LAST, 0)
         cast_group(nc.scalar.copy, LAST, 1)
+        cast_group(nc.scalar.copy, LAST, 2)
         cast_group(nc.scalar.copy, LAST, 3)
         quantize_group(LAST, 0)
-        cast_group(nc.vector.tensor_copy, LAST, 2)
         for c in range(0, 2):
             multiply(c, LAST, stop=True)
-        add_decayed(0)
         quantize_group(LAST, 1)
         for c in range(2, 4):
             multiply(c, LAST, stop=True)
+        add_decayed(0)
         add_decayed(1)
         store(0, 0, 2)
+        add_decayed(2)
         quantize_group(LAST, 2)
         for c in range(4, 8):
             multiply(c, LAST, stop=True)
-        add_decayed(2)
         add_decayed(3)
         store(1, 2, 4)
         quantize_group(LAST, 3)

@@ -46,7 +46,7 @@ def tile_mix_tied_ema_kernel(tc, x, de, dr, e, mom, out):
         narrow_scales = keep.tile([P, len(CHUNKS), H], U8, align_bytes=64)
         wide_codes = keep.tile([P, len(CHUNKS), D], U32, align_bytes=64)
         wide_scales = keep.tile([P, len(CHUNKS), D], U8, align_bytes=64)
-        result = keep.tile([P, D_TILES, H], F32)
+        result = keep.tile([P, D_TILES, H], F32, align_bytes=256)
         raw_narrow = {}
         raw_wide = {}
         grouped_narrow = {}
@@ -57,26 +57,23 @@ def tile_mix_tied_ema_kernel(tc, x, de, dr, e, mom, out):
             return operand[block * T_CHUNK : (block + 1) * T_CHUNK, :].rearrange("(p j) w -> p j w", j=PACK)
 
         def load_narrow(i):
-            narrow_raw = raw.tile([P, PACK, H], F32, name="narrow_raw")
-            nc.sync.dma_start(out=narrow_raw[:], in_=rows_of(i, products[CHUNKS[i][0]][2]))
+            narrow_raw = raw.tile([P, PACK, H], F32, name="narrow_raw", align_bytes=256)
+            nc.scalar.dma_start(out=narrow_raw[:], in_=rows_of(i, products[CHUNKS[i][0]][2]))
             raw_narrow[i] = narrow_raw
 
         def load_wide(i):
-            wide_raw = raw.tile([P, PACK, D], F32, name="wide_raw")
+            wide_raw = raw.tile([P, PACK, D], F32, name="wide_raw", align_bytes=256)
             nc.sync.dma_start(out=wide_raw[:], in_=rows_of(i, products[CHUNKS[i][0]][0]))
             raw_wide[i] = wide_raw
 
-        def group_rows(hbm, g):
-            c, n = GROUPS[g]
-            return hbm[c * P : (c + n) * P, :].rearrange("(c p) h -> p c h", c=n)
+        def tile_rows(hbm, c0, c1):
+            return hbm[c0 * P : c1 * P, :].rearrange("(c p) h -> p c h", p=P)
 
-        def load_mom(g):
-            c, n = GROUPS[g]
-            nc.sync.dma_start(out=result[:, c : c + n, :], in_=group_rows(mom, g))
+        def load_mom(c0, c1):
+            nc.sync.dma_start(out=result[:, c0:c1, :], in_=tile_rows(mom, c0, c1))
 
-        def store(g, c0, c1):
-            first = GROUPS[g][0]
-            nc.sync.dma_start(out=group_rows(out, g)[:, c0 - first : c1 - first, :], in_=result[:, c0:c1, :])
+        def store(c0, c1):
+            nc.sync.dma_start(out=tile_rows(out, c0, c1), in_=result[:, c0:c1, :])
 
         def interleave(copy, grouped, source):
             copy(
@@ -158,7 +155,7 @@ def tile_mix_tied_ema_kernel(tc, x, de, dr, e, mom, out):
             cast_wide(nc.scalar.copy, i, MAIN, D)
             cast_wide(nc.vector.tensor_copy, i, 0, MAIN)
             if i == 0:
-                load_mom(3)
+                load_mom(LAST_PAIR[0], LAST_PAIR[1] + 1)
             if i + RAW_BUFS <= LAST:
                 load_narrow(i + RAW_BUFS)
                 load_wide(i + RAW_BUFS)
@@ -182,40 +179,40 @@ def tile_mix_tied_ema_kernel(tc, x, de, dr, e, mom, out):
                 for c in FIRST_PAIR:
                     multiply(c, i)
 
-        for g in range(3):
-            load_mom(g)
+        for c, n in GROUPS[:-1]:
+            load_mom(c, c + n)
 
         cast_narrow(LAST)
         open_wide(LAST)
         quantize_narrow(LAST)
         cast_group(nc.vector.tensor_copy, LAST, 0)
-        cast_group(nc.scalar.copy, LAST, 1)
-        cast_group(nc.scalar.copy, LAST, 2)
-        cast_group(nc.scalar.copy, LAST, 3)
-        quantize_group(LAST, 0)
-        for c in range(0, 2):
+        for g in (1, 2, 3):
+            cast_group(nc.scalar.copy, LAST, g)
+        for g in range(2):
+            quantize_group(LAST, g)
+            c = GROUPS[g][0]
             multiply(c, LAST, stop=True)
-        quantize_group(LAST, 1)
-        for c in range(2, 4):
-            multiply(c, LAST, stop=True)
-        add_decayed(0)
-        add_decayed(1)
-        store(0, 0, 2)
+            multiply(c + 1, LAST, stop=True)
+        for c in FIRST_PAIR:
+            add_decayed(c)
+        store(FIRST_PAIR[0], FIRST_PAIR[1] + 1)
+        for c in LAST_PAIR:
+            acc[c] = bank(c - 8)
+            for i in range(SWAP + 1, LAST):
+                multiply(c, i, start=(i == SWAP + 1))
         add_decayed(2)
         quantize_group(LAST, 2)
         for c in range(4, 8):
             multiply(c, LAST, stop=True)
         add_decayed(3)
-        store(1, 2, 4)
+        store(2, 4)
         quantize_group(LAST, 3)
         for c in LAST_PAIR:
-            acc[c] = bank(c - 8)
-            for i in range(SWAP + 1, LAST + 1):
-                multiply(c, i, start=(i == SWAP + 1), stop=(i == LAST))
+            multiply(c, LAST, stop=True)
         for c in range(4, 8, 2):
             add_decayed(c)
             add_decayed(c + 1)
-            store(2, c, c + 2)
+            store(c, c + 2)
         for c in LAST_PAIR:
             add_rest(c)
-        store(3, 8, 10)
+        store(LAST_PAIR[0], LAST_PAIR[1] + 1)

from contextlib import ExitStack

import concourse.mybir as mybir

T, D, H = 2048, 1280, 512
FLOPS = 2 * 2 * T * D * H

F32 = mybir.dt.float32
BF16 = mybir.dt.bfloat16
U32 = mybir.dt.uint32
U8 = mybir.dt.uint8
E4M3 = mybir.dt.float8_e4m3fn_x4
E5M2 = mybir.dt.float8_e5m2_x4

P = 128
PACK = 4
T_CHUNK = P * PACK
BLOCKS = T // T_CHUNK
D_TILES = D // P
DECAY = 0.9
RAW_BUFS = 4

GROUPS = [(0, 2), (2, 2), (4, 4), (8, 2)]
FIRST_PAIR = [0, 1]
LAST_PAIR = [8, 9]
MIDDLE = list(range(2, 8))
MAIN = 8 * P

CHUNKS = [(product, block) for product in range(2) for block in range(BLOCKS)]
LAST = len(CHUNKS) - 1
SWAP = LAST - 2


def tile_mix_tied_ema_kernel(tc, x, de, dr, e, mom, out):
    nc = tc.nc
    products = [(x, E4M3, de, E5M2), (dr, E5M2, e, E4M3)]

    with ExitStack() as ctx:
        raw = ctx.enter_context(tc.tile_pool(name="raw", bufs=RAW_BUFS))
        stage = ctx.enter_context(tc.tile_pool(name="stage", bufs=2))
        keep = ctx.enter_context(tc.tile_pool(name="keep", bufs=1))
        psum = ctx.enter_context(tc.psum_pool(name="psum", bufs=1))
        ctx.enter_context(tc.manual_schedule())

        narrow_codes = keep.tile([P, len(CHUNKS), H], U32, align_bytes=64)
        narrow_scales = keep.tile([P, len(CHUNKS), H], U8, align_bytes=64)
        wide_codes = keep.tile([P, len(CHUNKS), D], U32, align_bytes=64)
        wide_scales = keep.tile([P, len(CHUNKS), D], U8, align_bytes=64)
        result = keep.tile([P, D_TILES, H], F32, align_bytes=256)
        raw_narrow = {}
        raw_wide = {}
        grouped_narrow = {}
        grouped_wide = {}

        def rows_of(i, operand):
            block = CHUNKS[i][1]
            return operand[block * T_CHUNK : (block + 1) * T_CHUNK, :].rearrange("(p j) w -> p j w", j=PACK)

        def load_narrow(i):
            narrow_raw = raw.tile([P, PACK, H], F32, name="narrow_raw", align_bytes=256)
            nc.scalar.dma_start(out=narrow_raw[:], in_=rows_of(i, products[CHUNKS[i][0]][2]))
            raw_narrow[i] = narrow_raw

        def load_wide(i):
            wide_raw = raw.tile([P, PACK, D], F32, name="wide_raw", align_bytes=256)
            nc.sync.dma_start(out=wide_raw[:], in_=rows_of(i, products[CHUNKS[i][0]][0]))
            raw_wide[i] = wide_raw

        def tile_rows(hbm, c0, c1):
            return hbm[c0 * P : c1 * P, :].rearrange("(c p) h -> p c h", p=P)

        def load_mom(c0, c1):
            nc.sync.dma_start(out=result[:, c0:c1, :], in_=tile_rows(mom, c0, c1))

        def store(c0, c1):
            nc.sync.dma_start(out=tile_rows(out, c0, c1), in_=result[:, c0:c1, :])

        def interleave(copy, grouped, source):
            copy(
                out=grouped.rearrange("p (q i) j -> p q j i", i=4),
                in_=source.rearrange("p j (q i) -> p q j i", i=4),
            )

        def cast_narrow(i):
            narrow_grouped = stage.tile([P, H, PACK], BF16, name="narrow_grouped", align_bytes=64)
            interleave(nc.scalar.copy, narrow_grouped[:], raw_narrow[i][:])
            grouped_narrow[i] = narrow_grouped

        def open_wide(i):
            wide_grouped = stage.tile([P, D, PACK], BF16, name="wide_grouped", align_bytes=64)
            grouped_wide[i] = wide_grouped

        def cast_wide(copy, i, w0, w1):
            interleave(copy, grouped_wide[i][:, w0:w1, :], raw_wide[i][:, :, w0:w1])

        def cast_group(copy, i, g):
            c, n = GROUPS[g]
            cast_wide(copy, i, c * P, (c + n) * P)

        def quantize(format_x4, codes, scales, grouped):
            nc.vector.quantize_mx(
                out=codes.bitcast(format_x4), scales=scales, in_=grouped.rearrange("p w j -> p (w j)")
            )

        def quantize_narrow(i):
            quantize(products[CHUNKS[i][0]][3], narrow_codes[:, i, :], narrow_scales[:, i, :], grouped_narrow[i][:])

        def quantize_wide(i, w0, w1):
            wide_format = products[CHUNKS[i][0]][1]
            quantize(wide_format, wide_codes[:, i, w0:w1], wide_scales[:, i, w0:w1], grouped_wide[i][:, w0:w1, :])

        def quantize_group(i, g):
            c, n = GROUPS[g]
            quantize_wide(i, c * P, (c + n) * P)

        def multiply(c, i, start=False, stop=False):
            wide, wide_format, narrow, narrow_format = products[CHUNKS[i][0]]
            d = slice(c * P, (c + 1) * P)
            nc.tensor.matmul_mx(
                out=acc[c][:],
                lhsT=wide_codes[:, i, d].bitcast(wide_format),
                lhsT_scale=wide_scales[:, i, d],
                rhs=narrow_codes[:, i, :].bitcast(narrow_format),
                rhs_scale=narrow_scales[:, i, :],
                start=start,
                stop=stop,
            )

        def bank(b):
            return psum.tile([P, H], F32, name="bank%d" % b)

        def add_decayed(c):
            nc.vector.scalar_tensor_tensor(
                out=result[:, c, :],
                in0=result[:, c, :],
                scalar=DECAY,
                in1=acc[c][:],
                op0=mybir.AluOpType.mult,
                op1=mybir.AluOpType.add,
            )

        def add_rest(c):
            nc.vector.tensor_add(out=result[:, c, :], in0=result[:, c, :], in1=acc[c][:])

        acc = {c: bank(c) for c in MIDDLE}
        for c in LAST_PAIR:
            acc[c] = bank(c - 8)
        for i in range(RAW_BUFS):
            load_narrow(i)
            load_wide(i)

        for i in range(LAST):
            cast_narrow(i)
            open_wide(i)
            cast_wide(nc.scalar.copy, i, MAIN, D)
            cast_wide(nc.vector.tensor_copy, i, 0, MAIN)
            if i == 0:
                load_mom(LAST_PAIR[0], LAST_PAIR[1] + 1)
            if i + RAW_BUFS <= LAST:
                load_narrow(i + RAW_BUFS)
                load_wide(i + RAW_BUFS)

            quantize_narrow(i)
            quantize_wide(i, MAIN, D)
            quantize_wide(i, 0, MAIN)
            if i <= SWAP:
                for c in LAST_PAIR:
                    multiply(c, i, start=(i == 0), stop=(i == SWAP))
            for c in MIDDLE:
                multiply(c, i, start=(i == 0))
            if i == SWAP:
                for c in LAST_PAIR:
                    add_decayed(c)
                for c in FIRST_PAIR:
                    acc[c] = bank(c)
                    for k in range(SWAP + 1):
                        multiply(c, k, start=(k == 0))
            if i > SWAP:
                for c in FIRST_PAIR:
                    multiply(c, i)

        for c, n in GROUPS[:-1]:
            load_mom(c, c + n)

        cast_narrow(LAST)
        open_wide(LAST)
        quantize_narrow(LAST)
        cast_group(nc.vector.tensor_copy, LAST, 0)
        for g in (1, 2, 3):
            cast_group(nc.scalar.copy, LAST, g)
        for g in range(2):
            quantize_group(LAST, g)
            c = GROUPS[g][0]
            multiply(c, LAST, stop=True)
            multiply(c + 1, LAST, stop=True)
        for c in FIRST_PAIR:
            add_decayed(c)
        store(FIRST_PAIR[0], FIRST_PAIR[1] + 1)
        for c in LAST_PAIR:
            acc[c] = bank(c - 8)
            for i in range(SWAP + 1, LAST):
                multiply(c, i, start=(i == SWAP + 1))
        add_decayed(2)
        quantize_group(LAST, 2)
        for c in range(4, 8):
            multiply(c, LAST, stop=True)
        add_decayed(3)
        store(2, 4)
        quantize_group(LAST, 3)
        for c in LAST_PAIR:
            multiply(c, LAST, stop=True)
        for c in range(4, 8, 2):
            add_decayed(c)
            add_decayed(c + 1)
            store(c, c + 2)
        for c in LAST_PAIR:
            add_rest(c)
        store(LAST_PAIR[0], LAST_PAIR[1] + 1)
